import numpy as np
import ml_dtypes


def mxq(x, axis, fmt="e4m3"):
    dtype, down = {"e4m3": (ml_dtypes.float8_e4m3fn, 7), "e5m2": (ml_dtypes.float8_e5m2, 14)}[fmt]
    v = np.moveaxis(np.asarray(x, np.float32).astype(ml_dtypes.bfloat16).astype(np.float64), axis, -1)
    blocks = v.reshape(v.shape[:-1] + (-1, 32))
    amax = np.abs(blocks).max(-1, keepdims=True)
    byte = np.maximum(np.where(amax > 0, np.frexp(amax)[1] - 1 + 127, 0) - down, 1)
    scale = np.exp2(byte - 127.0)
    codes = (blocks / scale).astype(np.float32).astype(dtype).astype(np.float64)
    return np.moveaxis((codes * scale).reshape(v.shape), -1, axis)


WIDE = False


def mx_kscale(k):
    if not WIDE:
        return np.ones(k)
    levels = np.array([10, -10, 5, -5, 0])
    if k % 512:
        return np.exp2(np.random.permutation(np.resize(levels, k // 32))).repeat(32)
    a = np.empty((k // 512, 16))
    for p in range(k // 512):
        a[p, :8] = np.random.permutation(np.resize(levels, 8))
        for g in range(8):
            far = levels[np.abs(levels - a[p, g]) >= 10]
            a[p, g + 8] = far[np.random.randint(len(far))]
    return np.exp2(a.ravel()).repeat(32)


def f64(x):
    return np.asarray(x).astype(np.float64)


def striped(idx):
    return np.tile(np.asarray(idx).reshape(-1, 16).T, (8, 1)).astype(np.uint16)


def unstriped(offs):
    return offs[:16].T.reshape(-1).astype(np.int64)


E2M1 = np.array([0.0, 0.5, 1.0, 1.5, 2.0, 3.0, 4.0, 6.0, -0.0, -0.5, -1.0, -1.5, -2.0, -3.0, -4.0, -6.0])


def pack_weight(w, fmt):
    k, n = w.shape
    w = f64(np.asarray(w, np.float32).astype(ml_dtypes.bfloat16)).reshape(k // 32, 32, n)
    amax = np.abs(w).max(1)
    if fmt == "e4m3":
        byte = np.frexp(amax)[1] - 1 + 127 - 7
    else:
        mant, ex = np.frexp(amax / 6.0)
        byte = np.where(mant > 0.5, ex, ex - 1) + 127
    byte = np.clip(np.where(amax > 0, byte, 1), 1, 254)
    scaled = (w * np.exp2(127.0 - byte)[:, None, :]).reshape(k, n).astype(np.float32)
    by_word = np.ascontiguousarray(scaled.reshape(k // 512, 128, 4, n).transpose(0, 1, 3, 2))
    if fmt == "e4m3":
        words = by_word.astype(ml_dtypes.float8_e4m3fn).view(np.uint8)
    else:
        c = by_word.astype(ml_dtypes.float4_e2m1fn).view(np.uint8) & 0xF
        words = (c[..., 0::2] | (c[..., 1::2] << 4)).reshape(k // 512, 128, 2 * n)
    return np.ascontiguousarray(words), np.ascontiguousarray(byte.astype(np.uint8).reshape(k // 512, 16, n))


def unpack_weight(words, scales, fmt):
    g, _, n = scales.shape
    words = np.ascontiguousarray(words).reshape(g, 128, n, -1)
    if fmt == "e4m3":
        vals = words.view(ml_dtypes.float8_e4m3fn).astype(np.float64)
    else:
        nib = np.empty((g, 128, n, 4), np.uint8)
        nib[..., 0::2] = words & 0xF
        nib[..., 1::2] = words >> 4
        vals = E2M1[nib]
    vals = vals * np.repeat(np.exp2(scales.astype(np.float64) - 127.0), 8, axis=1)[..., None]
    return vals.transpose(0, 1, 3, 2).reshape(g * 512, n)


def sigmoid(v):
    return 1.0 / (1.0 + np.exp(-v))


def bf(x):
    return np.asarray(x, np.float32).astype(ml_dtypes.bfloat16)


def planes(Y):
    r, m = Y.shape
    b = f64(bf(Y)).reshape(r // 32, 32, m)
    amax = np.abs(b).max(1)
    byte = np.clip(np.where(amax > 0, np.frexp(amax)[1] - 1 + 127 - 7, 1), 1, 254)
    codes = (b * np.exp2(127.0 - byte)[:, None, :]).reshape(r, m).astype(np.float32).astype(ml_dtypes.float8_e4m3fn).view(np.uint8)
    words = codes.reshape(r // 512, 128, 4, m).transpose(0, 1, 3, 2)
    return np.ascontiguousarray(words), np.ascontiguousarray(byte.astype(np.uint8).reshape(r // 512, 16, m))


D, E, T, I, Q, G = 512, 512, 2048, 512, 256, 32


def setup_inputs():
    n = np.random.standard_normal
    idx = np.random.permutation(T)[:I]
    fd = mx_kscale(D)
    fi = mx_kscale(I)
    ti = np.ones(T)
    ti[idx] = fi
    keysp = pack_weight(n((D, T)) / fd[:, None], "e2m1")
    return {
        "query": (n((D, Q)) * 0.7 / np.sqrt(D) * fd[:, None]).astype(np.float32),
        "dquery": (n((D, Q)) * 1.0 / np.sqrt(D) * fd[:, None]).astype(np.float32),
        "keys_words": keysp[0],
        "keys_scales": keysp[1],
        "th": (np.random.uniform(-0.2, 0.2, (Q, 1))).astype(np.float32),
        "steep": (np.random.uniform(2.0, 8.0, (Q, 1))).astype(np.float32),
        "os": (np.random.uniform(4.0, 16.0, (1, I)) * fi).astype(np.float32),
        "vals": (n((E, T)) / ti).astype(np.float32),
        "offs": striped(idx),
    }


def reference(query, dquery, keys_words, keys_scales, th, steep, os, vals, offs):
    idx = unstriped(offs)
    keysu = unpack_weight(keys_words, keys_scales, "e2m1")
    queryq = mxq(f64(query), 0, "e4m3")
    keysidxg = keysu[:, idx]
    a = queryq.T @ keysidxg
    dqueryq = mxq(f64(dquery), 0, "e4m3")
    ta = dqueryq.T @ keysidxg
    s = a.reshape(Q, G, I // G).mean(axis=2)
    gt = sigmoid((s - f64(th)) * f64(steep))
    gr = np.repeat(gt, I // G, axis=1)
    r = np.exp(a - np.max(a, axis=1, keepdims=True))
    p = r * gr
    ts = ta.reshape(Q, G, I // G).mean(axis=2)
    tgt = ts * f64(steep) * gt * (1.0 - gt)
    tgr = np.repeat(tgt, I // G, axis=1)
    tr = ta * r
    tp = tr * gr + tgr * r
    tw = (tp - np.sum(tp, axis=1, keepdims=True) * p / np.sum(p, axis=1, keepdims=True)) / np.sum(p, axis=1, keepdims=True)
    wo1 = tw * f64(os)
    wt1 = wo1.T
    vt1 = f64(vals)[:, idx].T
    vt1q = mxq(vt1, 0, "e4m3")
    wt1q = mxq(wt1, 0, "e4m3")
    o = vt1q.T @ wt1q
    words, scales = planes(o)
    return o, words, scales

@@ -1,0 +1,210 @@
+from contextlib import ExitStack
+
+import concourse.mybir as mybir
+from concourse.masks import make_identity
+
+D, E, T, I, Q, G = 512, 512, 2048, 512, 256, 32
+FLOPS = 2 * 2 * D * Q * I + 2 * I * E * Q
+
+F32 = mybir.dt.float32
+BF16 = mybir.dt.bfloat16
+I32 = mybir.dt.int32
+U32 = mybir.dt.uint32
+U16 = mybir.dt.uint16
+U8 = mybir.dt.uint8
+FP8X4 = mybir.dt.float8_e4m3fn_x4
+FP4X4 = mybir.dt.float4_e2m1fn_x4
+ALU = mybir.AluOpType
+ACT = mybir.ActivationFunctionType
+AXIS = mybir.AxisListType
+
+P = 128
+PACK = 4
+PAGE = I // G
+ROW_TILES = Q // P
+
+
+def tile_attend_ttpagegate_pl_kernel(tc, query, dquery, keys_words, keys_scales, th, steep, slot_factor, vals, offs, out_0, out_1, out_2):
+    nc = tc.nc
+    with ExitStack() as ctx:
+        sb = ctx.enter_context(tc.tile_pool(name="sb", bufs=1))
+        ps = ctx.enter_context(tc.psum_pool(name="ps", bufs=1))
+
+        offsets = sb.tile([P, I // 16], U16, name="offsets")
+        nc.sync.dma_start(offsets[:], offs)
+
+        byte_pool = sb.tile([P, T], U8, name="byte_pool")
+        nc.gpsimd.memset(byte_pool[:].bitcast(I32), 0)
+        for quad in range(4):
+            nc.sync.dma_start(byte_pool[:].bitcast(I32)[32 * quad : 32 * quad + 4, :], keys_scales[0].bitcast(I32)[4 * quad : 4 * quad + 4, :])
+        key_pool = sb.tile([P, T], U16, name="key_pool")
+        nc.sync.dma_start(key_pool[:].bitcast(I32), keys_words[0].bitcast(I32))
+
+        raw = []
+        for name, src in (("query", query), ("dquery", dquery)):
+            t_raw = sb.tile([P, PACK, Q], F32, name=name + "_raw")
+            nc.sync.dma_start(t_raw[:], src.rearrange("(p t) q -> p t q", t=PACK))
+            raw.append(t_raw)
+
+        th_sb = sb.tile([P, ROW_TILES], F32, name="th_sb")
+        steep_sb = sb.tile([P, ROW_TILES], F32, name="steep_sb")
+        os_sb = sb.tile([P, PACK], F32, name="os_sb")
+        with nc.allow_non_contiguous_dma(reason="one value of each row tile to a partition"):
+            nc.sync.dma_start(th_sb[:], th.rearrange("(k p) o -> p (k o)", p=P))
+            nc.sync.dma_start(steep_sb[:], steep.rearrange("(k p) o -> p (k o)", p=P))
+        nc.sync.dma_start(os_sb[:], slot_factor.rearrange("o (p t) -> p (o t)", t=PACK))
+
+        val_pool = []
+        for t in range(PACK):
+            v = sb.tile([P, T], F32, name=f"val_pool{t}")
+            nc.sync.dma_start(v[:], vals.rearrange("(p t) c -> p t c", t=PACK)[:, t, :])
+            val_pool.append(v)
+
+
+        warm = sb.tile([P, 1], F32, name="warm")
+        nc.gpsimd.memset(warm[:], 0.0)
+        warmed = sb.tile([P, 1], F32, name="warmed")
+        nc.scalar.activation(warmed[:], warm[:], ACT.Sigmoid)
+
+        ident = sb.tile([P, P], F32, name="ident")
+        make_identity(nc, ident[:])
+
+        key_words = sb.tile([P, I], U16, name="key_words", align_bytes=64)
+        key_bytes = sb.tile([P, I], U8, name="key_bytes", align_bytes=64)
+        nc.vector.tensor_copy(key_bytes[:], byte_pool[:].indirect(offsets[:]))
+        nc.vector.tensor_copy(key_words[:], key_pool[:].indirect(offsets[:]))
+
+        score = [[None, None], [None, None]]
+        for n in range(2):
+            for k in range(ROW_TILES):
+                grouped = sb.tile([P, P, PACK], BF16, name=f"q_grouped{n}{k}", align_bytes=64)
+                dst = grouped[:].rearrange("p (c i) t -> p c t i", i=4)
+                src = raw[n][:, :, k * P : (k + 1) * P].rearrange("p t (c i) -> p c t i", i=4)
+                if (n, k) == (1, 1):
+                    nc.vector.tensor_copy(dst, src)
+                else:
+                    nc.scalar.copy(dst, src)
+                codes = sb.tile([P, P], U32, name=f"q_codes{n}{k}", align_bytes=64)
+                scales = sb.tile([P, P], U8, name=f"q_scales{n}{k}", align_bytes=64)
+                nc.vector.quantize_mx(out=codes[:].bitcast(FP8X4), scales=scales[:], in_=grouped[:].rearrange("p q t -> p (q t)"))
+                bank = ps.tile([P, I], F32, name=f"score{n}{k}", tag=f"bank{n}{k}")
+                nc.tensor.matmul_mx(out=bank[:], lhsT=codes[:].bitcast(FP8X4), lhsT_scale=scales[:],
+                                    rhs=key_words[:].bitcast(FP4X4), rhs_scale=key_bytes[:], start=True, stop=True)
+                score[n][k] = bank
+        a, ta = score
+
+        slope = sb.tile([P, ROW_TILES], F32, name="slope")
+        nslope = sb.tile([P, ROW_TILES], F32, name="nslope")
+        shift = sb.tile([P, ROW_TILES], F32, name="shift")
+        nshift = sb.tile([P, ROW_TILES], F32, name="nshift")
+        nc.gpsimd.tensor_scalar(slope[:], steep_sb[:], 1.0 / PAGE, 0.0, ALU.mult, ALU.add)
+        nc.gpsimd.tensor_scalar(nslope[:], steep_sb[:], -1.0 / PAGE, 0.0, ALU.mult, ALU.add)
+        nc.gpsimd.tensor_tensor(shift[:], steep_sb[:], th_sb[:], ALU.mult)
+        nc.gpsimd.tensor_scalar(nshift[:], shift[:], -1.0, 0.0, ALU.mult, ALU.add)
+
+        gate, shut = [], []
+        page_sums = sb.tile([P, ROW_TILES, G], F32, name="page_sums", tag="sums_then_r")
+        for k in range(ROW_TILES):
+            s = page_sums[:, k, :]
+            nc.vector.tensor_reduce(s, a[k][:].rearrange("q (g j) -> q g j", j=PAGE), AXIS.X, ALU.add)
+            g4 = sb.tile([P, G, 4], F32, name=f"gate{k}")
+            nc.scalar.activation(g4[:], s.rearrange("q (g o) -> q g o", o=1).to_broadcast([P, G, 4]), ACT.Sigmoid, bias=nshift[:, k : k + 1], scale=slope[:, k : k + 1])
+            sh = sb.tile([P, G], F32, name=f"shut{k}")
+            nc.scalar.activation(sh[:], s, ACT.Sigmoid, bias=shift[:, k : k + 1], scale=nslope[:, k : k + 1])
+            gate.append(g4)
+            shut.append(sh)
+
+        r = []
+        r_all = sb.tile([P, ROW_TILES, PACK, P], F32, name="r_all", tag="sums_then_r")
+        for k in range(ROW_TILES):
+            negmax = sb.tile([P, 1], F32, name=f"negmax{k}")
+            nc.vector.tensor_reduce(negmax[:], a[k][:], AXIS.X, ALU.max, negate=True)
+            rk = r_all[:, k, :, :]
+            nc.scalar.activation(rk, a[k][:].rearrange("q (p t) -> q t p", t=PACK), ACT.Exp, bias=negmax[:])
+            r.append(rk)
+
+        def over_places(x):
+            return x.rearrange("q g j -> q (g j)").rearrange("q (o p) -> q o p", o=1).to_broadcast([P, PACK, P])
+
+        v_codes = sb.tile([P, E], U32, name="v_codes", align_bytes=64)
+        v_scales = sb.tile([P, E], U8, name="v_scales", align_bytes=64)
+
+        def values(t):
+            picked = sb.tile([P, I], BF16, name=f"picked{t}", tag=f"then_picked{t}")
+            nc.vector.tensor_copy(picked[:], val_pool[t][:].indirect(offsets[:]))
+            pairs = picked[:].bitcast(F32)
+            turned = ps.tile([P, 2, P], F32, name=f"v_turned{t}", tag=f"vbank{t}")
+            for u in range(2):
+                nc.tensor.transpose(turned[:, u, :], pairs[:, u : I // 2 : 2], ident[:])
+            grouped = sb.tile([P, P, PACK], BF16, name=f"v_grouped{t}", align_bytes=64)
+            nc.scalar.copy(grouped[:].bitcast(F32), turned[:].rearrange("p u e -> p e u"))
+            nc.vector.quantize_mx(out=v_codes[:, t * P : (t + 1) * P].bitcast(FP8X4), scales=v_scales[:, t * P : (t + 1) * P], in_=grouped[:].rearrange("p e t -> p (e t)"))
+
+        def weights(k):
+            ts = sb.tile([P, G], F32, name=f"ts{k}")
+            nc.vector.tensor_reduce(ts[:], ta[k][:].rearrange("q (g j) -> q g j", j=PAGE), AXIS.X, ALU.add)
+            h = sb.tile([P, G, 4], F32, name=f"h{k}", tag="then_picked0" if k == 0 else "h1")
+            nc.vector.scalar_tensor_tensor(h[:], ts[:].rearrange("q (g o) -> q g o", o=1).to_broadcast([P, G, 4]), slope[:, k : k + 1],
+                                           shut[k][:].rearrange("q (g o) -> q g o", o=1).to_broadcast([P, G, 4]), ALU.mult, ALU.mult)
+            zk = sb.tile([P, PACK, P], F32, name=f"z{k}", tag=f"then_picked{k + 1}")
+            nc.vector.tensor_tensor(zk[:], ta[k][:].rearrange("q (p t) -> q t p", t=PACK), over_places(h[:]), ALU.add)
+            p = sb.tile([P, PACK, P], F32, name=f"p{k}")
+            total = sb.tile([P, 1], F32, name=f"total{k}")
+            nc.vector.scalar_tensor_tensor(p[:], r[k], 1.0, over_places(gate[k][:]), ALU.mult, ALU.mult, accum_out=total[:])
+            inv = sb.tile([P, 1], F32, name=f"inv{k}", tag="inv0" if k == 0 else "then_picked3")
+            nc.vector.reciprocal(inv[:], total[:])
+            tp = sb.tile([P, PACK, P], F32, name=f"tp{k}")
+            mean = sb.tile([P, 1], F32, name=f"mean{k}")
+            nc.vector.scalar_tensor_tensor(tp[:], p[:], inv[:], zk[:], ALU.mult, ALU.mult, accum_out=mean[:])
+            ninv = sb.tile([P, 1], F32, name=f"ninv{k}")
+            nc.scalar.activation(ninv[:], inv[:], ACT.Copy, scale=-1.0)
+            back = sb.tile([P, 1], F32, name=f"back{k}")
+            nc.scalar.activation(back[:], mean[:], ACT.Copy, scale=ninv[:])
+            pk = sb.tile([P, PACK, P], F32, name=f"pk{k}")
+            nc.scalar.activation(pk[:], p[:], ACT.Copy, scale=back[:])
+            turned = ps.tile([P, PACK, P], F32, name=f"w_turned{k}", tag=f"bank0{k}")
+            for t in range(PACK):
+                nc.tensor.matmul(turned[:, t, :], tp[:, t, :], ident[:], start=True, stop=False, is_transpose=True)
+                nc.tensor.matmul(turned[:, t, :], pk[:, t, :], ident[:], start=False, stop=True, is_transpose=True)
+            grouped = sb.tile([P, P, PACK], BF16, name=f"w_grouped{k}", align_bytes=64)
+            if k == 0:
+                scaled = sb.tile([P, PACK, P], BF16, name=f"w_scaled{k}")
+                for t in range(PACK):
+                    nc.scalar.activation(scaled[:, t, :], turned[:, t, :], ACT.Copy, scale=os_sb[:, t : t + 1])
+                nc.scalar.copy(grouped[:].rearrange("p (c i) t -> p c t i", i=4), scaled[:].rearrange("p t (c i) -> p c t i", i=4))
+            else:
+                nc.vector.tensor_tensor(grouped[:], turned[:].rearrange("p t q -> p q t"),
+                                        os_sb[:].rearrange("p (o t) -> p o t", o=1).to_broadcast([P, P, PACK]), ALU.mult)
+            codes = sb.tile([P, P], U32, name=f"w_codes{k}", align_bytes=64)
+            scales = sb.tile([P, P], U8, name=f"w_scales{k}", align_bytes=64)
+            nc.vector.quantize_mx(out=codes[:].bitcast(FP8X4), scales=scales[:], in_=grouped[:].rearrange("p q t -> p (q t)"))
+            return codes, scales
+
+        w = [weights(k) for k in range(ROW_TILES)]
+        for t in range(PACK):
+            values(t)
+
+        o_codes = sb.tile([P, Q], U32, name="o_codes", align_bytes=64)
+        o_scales = sb.tile([P, Q], U8, name="o_scales", align_bytes=64)
+        for k in range(ROW_TILES):
+            codes, scales = w[k]
+            rows = slice(k * P, (k + 1) * P)
+            o = sb.tile([P, PACK, P], F32, name=f"o{k}")
+            early = 3 if k == 0 else 2
+            for first, last, tag in ((0, early, f"bank1{k}"), (early, PACK, f"vbank{k}")):
+                acc = ps.tile([P, last - first, P], F32, name=f"acc{k}{first}", tag=tag)
+                for t in range(first, last):
+                    nc.tensor.matmul_mx(out=acc[:, t - first, :], lhsT=v_codes[:, t * P : (t + 1) * P].bitcast(FP8X4), lhsT_scale=v_scales[:, t * P : (t + 1) * P],
+                                        rhs=codes[:].bitcast(FP8X4), rhs_scale=scales[:], start=True, stop=True)
+                if (k, first) == (1, 0):
+                    nc.vector.tensor_copy(o[:, first:last, :], acc[:])
+                else:
+                    nc.scalar.copy(o[:, first:last, :], acc[:])
+            nc.sync.dma_start(out_0.rearrange("(p t) q -> p t q", t=PACK)[:, :, rows], o[:])
+            grouped = sb.tile([P, P, PACK], BF16, name=f"o_grouped{k}", align_bytes=64)
+            nc.vector.tensor_copy(grouped[:].rearrange("p (c i) t -> p c t i", i=4), o[:].rearrange("p t (c i) -> p c t i", i=4))
+            nc.vector.quantize_mx(out=o_codes[:, rows].bitcast(FP8X4), scales=o_scales[:, rows], in_=grouped[:].rearrange("p q t -> p (q t)"))
+        nc.sync.dma_start(out_1[0].rearrange("p q t -> p (q t)").bitcast(I32), o_codes[:].bitcast(I32))
+        for quad in range(4):
+            eng = nc.sync if quad % 2 == 0 else nc.scalar
+            eng.dma_start(out_2[0].bitcast(I32)[4 * quad : 4 * quad + 4, :], o_scales[:].bitcast(I32)[32 * quad : 32 * quad + 4, :])

@@ -29,6 +29,7 @@ def tile_attend_ttpagegate_pl_kernel(tc, query, dquery, keys_words, keys_scales,
     with ExitStack() as ctx:
         sb = ctx.enter_context(tc.tile_pool(name="sb", bufs=1))
         ps = ctx.enter_context(tc.psum_pool(name="ps", bufs=1))
+        vp = ctx.enter_context(tc.tile_pool(name="vp", bufs=1))
 
         offsets = sb.tile([P, I // 16], U16, name="offsets")
         nc.sync.dma_start(offsets[:], offs)
@@ -52,14 +53,16 @@ def tile_attend_ttpagegate_pl_kernel(tc, query, dquery, keys_words, keys_scales,
         with nc.allow_non_contiguous_dma(reason="one value of each row tile to a partition"):
             nc.sync.dma_start(th_sb[:], th.rearrange("(k p) o -> p (k o)", p=P))
             nc.sync.dma_start(steep_sb[:], steep.rearrange("(k p) o -> p (k o)", p=P))
-        nc.sync.dma_start(os_sb[:], slot_factor.rearrange("o (p t) -> p (o t)", t=PACK))
 
         val_pool = []
         for t in range(PACK):
-            v = sb.tile([P, T], F32, name=f"val_pool{t}")
-            nc.sync.dma_start(v[:], vals.rearrange("(p t) c -> p t c", t=PACK)[:, t, :])
+            v = vp.tile([P, T], F32, name=f"val_pool{t}", offset=4 * T * t, align_bytes=64)
+            for half in range(2 if t == 0 else 1):
+                cols = slice(half * T // 2, (half + 1) * T // 2) if t == 0 else slice(0, T)
+                nc.sync.dma_start(v[:, cols], vals.rearrange("(p t) c -> p t c", t=PACK)[:, t, cols])
+            if t == 0:
+                nc.sync.dma_start(os_sb[:], slot_factor.rearrange("o (p t) -> p (o t)", t=PACK))
             val_pool.append(v)
-
 
         warm = sb.tile([P, 1], F32, name="warm")
         nc.gpsimd.memset(warm[:], 0.0)
@@ -117,7 +120,7 @@ def tile_attend_ttpagegate_pl_kernel(tc, query, dquery, keys_words, keys_scales,
         r = []
         r_all = sb.tile([P, ROW_TILES, PACK, P], F32, name="r_all", tag="sums_then_r")
         for k in range(ROW_TILES):
-            negmax = sb.tile([P, 1], F32, name=f"negmax{k}")
+            negmax = sb.tile([P, 1], F32, name=f"negmax{k}", tag="negmax0" if k == 0 else "then_picked0")
             nc.vector.tensor_reduce(negmax[:], a[k][:], AXIS.X, ALU.max, negate=True)
             rk = r_all[:, k, :, :]
             nc.scalar.activation(rk, a[k][:].rearrange("q (p t) -> q t p", t=PACK), ACT.Exp, bias=negmax[:])
@@ -126,28 +129,48 @@ def tile_attend_ttpagegate_pl_kernel(tc, query, dquery, keys_words, keys_scales,
         def over_places(x):
             return x.rearrange("q g j -> q (g j)").rearrange("q (o p) -> q o p", o=1).to_broadcast([P, PACK, P])
 
-        v_codes = sb.tile([P, E], U32, name="v_codes", align_bytes=64)
-        v_scales = sb.tile([P, E], U8, name="v_scales", align_bytes=64)
+        def after_gather(t, place, shape, dtype, name):
+            return vp.tile(shape, dtype, name=name, offset=4 * T * t + 2048 * place, align_bytes=64)
+
+        early_in = sb.tile([P, 4 * I], BF16, name="early_in", align_bytes=64)
+        late_in = after_gather(3, 1, [P, 2 * I], BF16, "late_in")
+        early_codes = after_gather(3, 0, [P, 4 * P], U32, "early_codes")
+        late_codes = sb.tile([P, 2 * P], U32, name="late_codes", align_bytes=64)
+        early_scales = sb.tile([P, 4 * P], U8, name="early_scales", align_bytes=64)
+        late_scales = sb.tile([P, 2 * P], U8, name="late_scales", align_bytes=64)
+
+        def operand(group, n):
+            bf, codes, scales = group
+            return bf[:, n * I : (n + 1) * I].rearrange("p (c t) -> p c t", t=PACK), codes[:, n * P : (n + 1) * P].bitcast(FP8X4), scales[:, n * P : (n + 1) * P]
+
+        early, late = (early_in, early_codes, early_scales), (late_in, late_codes, late_scales)
+        v_op = [operand(early, 0), operand(early, 1), operand(early, 2), operand(late, 0)]
+        w_op = [operand(early, 3), operand(late, 1)]
 
         def values(t):
             picked = sb.tile([P, I], BF16, name=f"picked{t}", tag=f"then_picked{t}")
-            nc.vector.tensor_copy(picked[:], val_pool[t][:].indirect(offsets[:]))
+            if t == 0:
+                rounded = sb.tile([P, T], BF16, name="rounded")
+                for half in range(2):
+                    cols = slice(half * T // 2, (half + 1) * T // 2)
+                    nc.scalar.copy(rounded[:, cols], val_pool[t][:, cols])
+                nc.scalar.activation(picked[:], rounded[:].indirect(offsets[:]), ACT.Copy)
+            else:
+                nc.vector.tensor_copy(picked[:], val_pool[t][:].indirect(offsets[:]))
             pairs = picked[:].bitcast(F32)
             turned = ps.tile([P, 2, P], F32, name=f"v_turned{t}", tag=f"vbank{t}")
             for u in range(2):
                 nc.tensor.transpose(turned[:, u, :], pairs[:, u : I // 2 : 2], ident[:])
-            grouped = sb.tile([P, P, PACK], BF16, name=f"v_grouped{t}", align_bytes=64)
-            nc.scalar.copy(grouped[:].bitcast(F32), turned[:].rearrange("p u e -> p e u"))
-            nc.vector.quantize_mx(out=v_codes[:, t * P : (t + 1) * P].bitcast(FP8X4), scales=v_scales[:, t * P : (t + 1) * P], in_=grouped[:].rearrange("p e t -> p (e t)"))
+            nc.scalar.copy(v_op[t][0].bitcast(F32), turned[:].rearrange("p u e -> p e u"))
 
         def weights(k):
             ts = sb.tile([P, G], F32, name=f"ts{k}")
             nc.vector.tensor_reduce(ts[:], ta[k][:].rearrange("q (g j) -> q g j", j=PAGE), AXIS.X, ALU.add)
-            h = sb.tile([P, G, 4], F32, name=f"h{k}", tag="then_picked0" if k == 0 else "h1")
-            nc.vector.scalar_tensor_tensor(h[:], ts[:].rearrange("q (g o) -> q g o", o=1).to_broadcast([P, G, 4]), slope[:, k : k + 1],
-                                           shut[k][:].rearrange("q (g o) -> q g o", o=1).to_broadcast([P, G, 4]), ALU.mult, ALU.mult)
+            h = sb.tile([P, G], F32, name=f"h{k}")
+            nc.vector.scalar_tensor_tensor(h[:], ts[:], slope[:, k : k + 1], shut[k][:], ALU.mult, ALU.mult)
             zk = sb.tile([P, PACK, P], F32, name=f"z{k}", tag=f"then_picked{k + 1}")
-            nc.vector.tensor_tensor(zk[:], ta[k][:].rearrange("q (p t) -> q t p", t=PACK), over_places(h[:]), ALU.add)
+            nc.vector.tensor_tensor(zk[:].rearrange("q t (g j) -> q t g j", j=4), ta[k][:].rearrange("q (g j t) -> q t g j", t=PACK, j=4),
+                                    h[:].rearrange("q (a g b) -> q a g b", a=1, b=1).to_broadcast([P, PACK, G, 4]), ALU.add)
             p = sb.tile([P, PACK, P], F32, name=f"p{k}")
             total = sb.tile([P, 1], F32, name=f"total{k}")
             nc.vector.scalar_tensor_tensor(p[:], r[k], 1.0, over_places(gate[k][:]), ALU.mult, ALU.mult, accum_out=total[:])
@@ -156,6 +179,9 @@ def tile_attend_ttpagegate_pl_kernel(tc, query, dquery, keys_words, keys_scales,
             tp = sb.tile([P, PACK, P], F32, name=f"tp{k}")
             mean = sb.tile([P, 1], F32, name=f"mean{k}")
             nc.vector.scalar_tensor_tensor(tp[:], p[:], inv[:], zk[:], ALU.mult, ALU.mult, accum_out=mean[:])
+            return p, inv, tp, mean
+
+        def turn_weights(k, p, inv, tp, mean):
             ninv = sb.tile([P, 1], F32, name=f"ninv{k}")
             nc.scalar.activation(ninv[:], inv[:], ACT.Copy, scale=-1.0)
             back = sb.tile([P, 1], F32, name=f"back{k}")
@@ -166,36 +192,32 @@ def tile_attend_ttpagegate_pl_kernel(tc, query, dquery, keys_words, keys_scales,
             for t in range(PACK):
                 nc.tensor.matmul(turned[:, t, :], tp[:, t, :], ident[:], start=True, stop=False, is_transpose=True)
                 nc.tensor.matmul(turned[:, t, :], pk[:, t, :], ident[:], start=False, stop=True, is_transpose=True)
-            grouped = sb.tile([P, P, PACK], BF16, name=f"w_grouped{k}", align_bytes=64)
             if k == 0:
                 scaled = sb.tile([P, PACK, P], BF16, name=f"w_scaled{k}")
                 for t in range(PACK):
                     nc.scalar.activation(scaled[:, t, :], turned[:, t, :], ACT.Copy, scale=os_sb[:, t : t + 1])
-                nc.scalar.copy(grouped[:].rearrange("p (c i) t -> p c t i", i=4), scaled[:].rearrange("p t (c i) -> p c t i", i=4))
-            else:
-                nc.vector.tensor_tensor(grouped[:], turned[:].rearrange("p t q -> p q t"),
-                                        os_sb[:].rearrange("p (o t) -> p o t", o=1).to_broadcast([P, P, PACK]), ALU.mult)
-            codes = sb.tile([P, P], U32, name=f"w_codes{k}", align_bytes=64)
-            scales = sb.tile([P, P], U8, name=f"w_scales{k}", align_bytes=64)
-            nc.vector.quantize_mx(out=codes[:].bitcast(FP8X4), scales=scales[:], in_=grouped[:].rearrange("p q t -> p (q t)"))
-            return codes, scales
+                nc.scalar.copy(w_op[k][0].rearrange("p (c i) t -> p c t i", i=4), scaled[:].rearrange("p t (c i) -> p c t i", i=4))
+            return turned
 
-        w = [weights(k) for k in range(ROW_TILES)]
+        turned_w = [turn_weights(k, *weights(k)) for k in range(ROW_TILES)]
         for t in range(PACK):
             values(t)
+        nc.vector.tensor_tensor(w_op[1][0], turned_w[1][:].rearrange("p t q -> p q t"),
+                                os_sb[:].rearrange("p (o t) -> p o t", o=1).to_broadcast([P, P, PACK]), ALU.mult)
+        for bf, codes, scales in (early, late):
+            nc.vector.quantize_mx(out=codes[:].bitcast(FP8X4), scales=scales[:], in_=bf[:])
 
         o_codes = sb.tile([P, Q], U32, name="o_codes", align_bytes=64)
         o_scales = sb.tile([P, Q], U8, name="o_scales", align_bytes=64)
         for k in range(ROW_TILES):
-            codes, scales = w[k]
             rows = slice(k * P, (k + 1) * P)
             o = sb.tile([P, PACK, P], F32, name=f"o{k}")
-            early = 3 if k == 0 else 2
-            for first, last, tag in ((0, early, f"bank1{k}"), (early, PACK, f"vbank{k}")):
+            cut = 3 if k == 0 else 2
+            for first, last, tag in ((0, cut, f"bank1{k}"), (cut, PACK, f"vbank{k}")):
                 acc = ps.tile([P, last - first, P], F32, name=f"acc{k}{first}", tag=tag)
                 for t in range(first, last):
-                    nc.tensor.matmul_mx(out=acc[:, t - first, :], lhsT=v_codes[:, t * P : (t + 1) * P].bitcast(FP8X4), lhsT_scale=v_scales[:, t * P : (t + 1) * P],
-                                        rhs=codes[:].bitcast(FP8X4), rhs_scale=scales[:], start=True, stop=True)
+                    nc.tensor.matmul_mx(out=acc[:, t - first, :], lhsT=v_op[t][1], lhsT_scale=v_op[t][2],
+                                        rhs=w_op[k][1], rhs_scale=w_op[k][2], start=True, stop=True)
                 if (k, first) == (1, 0):
                     nc.vector.tensor_copy(o[:, first:last, :], acc[:])
                 else:

@@ -29,6 +29,7 @@ def tile_attend_ttpagegate_pl_kernel(tc, query, dquery, keys_words, keys_scales,
     with ExitStack() as ctx:
         sb = ctx.enter_context(tc.tile_pool(name="sb", bufs=1))
         ps = ctx.enter_context(tc.psum_pool(name="ps", bufs=1))
+        zp = ctx.enter_context(tc.tile_pool(name="zp", bufs=1))
         vp = ctx.enter_context(tc.tile_pool(name="vp", bufs=1))
 
         offsets = sb.tile([P, I // 16], U16, name="offsets")
@@ -41,28 +42,27 @@ def tile_attend_ttpagegate_pl_kernel(tc, query, dquery, keys_words, keys_scales,
         key_pool = sb.tile([P, T], U16, name="key_pool")
         nc.sync.dma_start(key_pool[:].bitcast(I32), keys_words[0].bitcast(I32))
 
+        row_numbers = sb.tile([P, P], F32, name="row_numbers")
+        nc.vector.memset(row_numbers[:], 0.0)
+        nc.sync.dma_start(row_numbers[0:2, :], th.rearrange("(k p) o -> k (p o)", p=P))
+        nc.sync.dma_start(row_numbers[2:4, :], steep.rearrange("(k p) o -> k (p o)", p=P))
+
         raw = []
         for name, src in (("query", query), ("dquery", dquery)):
             t_raw = sb.tile([P, PACK, Q], F32, name=name + "_raw")
             nc.sync.dma_start(t_raw[:], src.rearrange("(p t) q -> p t q", t=PACK))
             raw.append(t_raw)
 
-        th_sb = sb.tile([P, ROW_TILES], F32, name="th_sb")
-        steep_sb = sb.tile([P, ROW_TILES], F32, name="steep_sb")
         os_sb = sb.tile([P, PACK], F32, name="os_sb")
-        with nc.allow_non_contiguous_dma(reason="one value of each row tile to a partition"):
-            nc.sync.dma_start(th_sb[:], th.rearrange("(k p) o -> p (k o)", p=P))
-            nc.sync.dma_start(steep_sb[:], steep.rearrange("(k p) o -> p (k o)", p=P))
-
-        val_pool = []
-        for t in range(PACK):
-            v = vp.tile([P, T], F32, name=f"val_pool{t}", offset=4 * T * t, align_bytes=64)
-            for half in range(2 if t == 0 else 1):
-                cols = slice(half * T // 2, (half + 1) * T // 2) if t == 0 else slice(0, T)
-                nc.sync.dma_start(v[:, cols], vals.rearrange("(p t) c -> p t c", t=PACK)[:, t, cols])
-            if t == 0:
-                nc.sync.dma_start(os_sb[:], slot_factor.rearrange("o (p t) -> p (o t)", t=PACK))
-            val_pool.append(v)
+        val_rows = vals.rearrange("(p t) c -> p t c", t=PACK)
+        val_pool = [vp.tile([P, T], F32, name=f"val_pool{t}", offset=4 * T * t, align_bytes=64) for t in range(PACK)]
+        halves = [slice(0, T // 2), slice(T // 2, T)]
+        nc.sync.dma_start(val_pool[0][:, halves[0]], val_rows[:, 0, halves[0]])
+        nc.sync.dma_start(val_pool[1][:], val_rows[:, 1, :])
+        nc.sync.dma_start(val_pool[0][:, halves[1]], val_rows[:, 0, halves[1]])
+        nc.sync.dma_start(os_sb[:], slot_factor.rearrange("o (p t) -> p (o t)", t=PACK))
+        for t in range(2, PACK):
+            nc.sync.dma_start(val_pool[t][:], val_rows[:, t, :])
 
         warm = sb.tile([P, 1], F32, name="warm")
         nc.gpsimd.memset(warm[:], 0.0)
@@ -71,6 +71,19 @@ def tile_attend_ttpagegate_pl_kernel(tc, query, dquery, keys_words, keys_scales,
 
         ident = sb.tile([P, P], F32, name="ident")
         make_identity(nc, ident[:])
+
+        numbers = ps.tile([P, P], F32, name="numbers", tag="vbank0")
+        nc.tensor.transpose(numbers[:], row_numbers[:], ident[:])
+        slope = sb.tile([P, ROW_TILES], F32, name="slope")
+        nslope = sb.tile([P, ROW_TILES], F32, name="nslope")
+        th_sb = sb.tile([P, ROW_TILES], F32, name="th_sb")
+        nc.scalar.activation(slope[:], numbers[:, 2:4], ACT.Copy, scale=1.0 / PAGE)
+        nc.scalar.activation(nslope[:], numbers[:, 2:4], ACT.Copy, scale=-1.0 / PAGE)
+        nc.scalar.activation(th_sb[:], numbers[:, 0:2], ACT.Copy, scale=float(PAGE))
+        shift = sb.tile([P, ROW_TILES], F32, name="shift")
+        nshift = sb.tile([P, ROW_TILES], F32, name="nshift")
+        nc.vector.tensor_tensor(shift[:], slope[:], th_sb[:], ALU.mult)
+        nc.vector.tensor_tensor(nshift[:], nslope[:], th_sb[:], ALU.mult)
 
         key_words = sb.tile([P, I], U16, name="key_words", align_bytes=64)
         key_bytes = sb.tile([P, I], U8, name="key_bytes", align_bytes=64)
@@ -95,15 +108,6 @@ def tile_attend_ttpagegate_pl_kernel(tc, query, dquery, keys_words, keys_scales,
                                     rhs=key_words[:].bitcast(FP4X4), rhs_scale=key_bytes[:], start=True, stop=True)
                 score[n][k] = bank
         a, ta = score
-
-        slope = sb.tile([P, ROW_TILES], F32, name="slope")
-        nslope = sb.tile([P, ROW_TILES], F32, name="nslope")
-        shift = sb.tile([P, ROW_TILES], F32, name="shift")
-        nshift = sb.tile([P, ROW_TILES], F32, name="nshift")
-        nc.gpsimd.tensor_scalar(slope[:], steep_sb[:], 1.0 / PAGE, 0.0, ALU.mult, ALU.add)
-        nc.gpsimd.tensor_scalar(nslope[:], steep_sb[:], -1.0 / PAGE, 0.0, ALU.mult, ALU.add)
-        nc.gpsimd.tensor_tensor(shift[:], steep_sb[:], th_sb[:], ALU.mult)
-        nc.gpsimd.tensor_scalar(nshift[:], shift[:], -1.0, 0.0, ALU.mult, ALU.add)
 
         gate, shut = [], []
         page_sums = sb.tile([P, ROW_TILES, G], F32, name="page_sums", tag="sums_then_r")
@@ -148,11 +152,13 @@ def tile_attend_ttpagegate_pl_kernel(tc, query, dquery, keys_words, keys_scales,
         w_op = [operand(early, 3), operand(late, 1)]
 
         def values(t):
-            picked = sb.tile([P, I], BF16, name=f"picked{t}", tag=f"then_picked{t}")
+            if t in (1, 2):
+                picked = zp.tile([P, I], BF16, name=f"picked{t}", offset=2048 + 1024 * (t - 1))
+            else:
+                picked = sb.tile([P, I], BF16, name=f"picked{t}", tag=f"then_picked{t}")
             if t == 0:
                 rounded = sb.tile([P, T], BF16, name="rounded")
-                for half in range(2):
-                    cols = slice(half * T // 2, (half + 1) * T // 2)
+                for cols in halves:
                     nc.scalar.copy(rounded[:, cols], val_pool[t][:, cols])
                 nc.scalar.activation(picked[:], rounded[:].indirect(offsets[:]), ACT.Copy)
             else:
@@ -168,7 +174,7 @@ def tile_attend_ttpagegate_pl_kernel(tc, query, dquery, keys_words, keys_scales,
             nc.vector.tensor_reduce(ts[:], ta[k][:].rearrange("q (g j) -> q g j", j=PAGE), AXIS.X, ALU.add)
             h = sb.tile([P, G], F32, name=f"h{k}")
             nc.vector.scalar_tensor_tensor(h[:], ts[:], slope[:, k : k + 1], shut[k][:], ALU.mult, ALU.mult)
-            zk = sb.tile([P, PACK, P], F32, name=f"z{k}", tag=f"then_picked{k + 1}")
+            zk = zp.tile([P, PACK, P], F32, name=f"z{k}", offset=2048 * k)
             nc.vector.tensor_tensor(zk[:].rearrange("q t (g j) -> q t g j", j=4), ta[k][:].rearrange("q (g j t) -> q t g j", t=PACK, j=4),
                                     h[:].rearrange("q (a g b) -> q a g b", a=1, b=1).to_broadcast([P, PACK, G, 4]), ALU.add)
             p = sb.tile([P, PACK, P], F32, name=f"p{k}")

@@ -60,9 +60,9 @@ def tile_attend_ttpagegate_pl_kernel(tc, query, dquery, keys_words, keys_scales,
         nc.sync.dma_start(val_pool[0][:, halves[0]], val_rows[:, 0, halves[0]])
         nc.sync.dma_start(val_pool[1][:], val_rows[:, 1, :])
         nc.sync.dma_start(val_pool[0][:, halves[1]], val_rows[:, 0, halves[1]])
-        nc.sync.dma_start(os_sb[:], slot_factor.rearrange("o (p t) -> p (o t)", t=PACK))
         for t in range(2, PACK):
             nc.sync.dma_start(val_pool[t][:], val_rows[:, t, :])
+        nc.sync.dma_start(os_sb[:], slot_factor.rearrange("o (p t) -> p (o t)", t=PACK))
 
         warm = sb.tile([P, 1], F32, name="warm")
         nc.gpsimd.memset(warm[:], 0.0)
@@ -198,18 +198,14 @@ def tile_attend_ttpagegate_pl_kernel(tc, query, dquery, keys_words, keys_scales,
             for t in range(PACK):
                 nc.tensor.matmul(turned[:, t, :], tp[:, t, :], ident[:], start=True, stop=False, is_transpose=True)
                 nc.tensor.matmul(turned[:, t, :], pk[:, t, :], ident[:], start=False, stop=True, is_transpose=True)
-            if k == 0:
-                scaled = sb.tile([P, PACK, P], BF16, name=f"w_scaled{k}")
-                for t in range(PACK):
-                    nc.scalar.activation(scaled[:, t, :], turned[:, t, :], ACT.Copy, scale=os_sb[:, t : t + 1])
-                nc.scalar.copy(w_op[k][0].rearrange("p (c i) t -> p c t i", i=4), scaled[:].rearrange("p t (c i) -> p c t i", i=4))
             return turned
 
         turned_w = [turn_weights(k, *weights(k)) for k in range(ROW_TILES)]
         for t in range(PACK):
             values(t)
-        nc.vector.tensor_tensor(w_op[1][0], turned_w[1][:].rearrange("p t q -> p q t"),
-                                os_sb[:].rearrange("p (o t) -> p o t", o=1).to_broadcast([P, P, PACK]), ALU.mult)
+        for k in range(ROW_TILES):
+            nc.vector.tensor_tensor(w_op[k][0], turned_w[k][:].rearrange("p t q -> p q t"),
+                                    os_sb[:].rearrange("p (o t) -> p o t", o=1).to_broadcast([P, P, PACK]), ALU.mult)
         for bf, codes, scales in (early, late):
             nc.vector.quantize_mx(out=codes[:].bitcast(FP8X4), scales=scales[:], in_=bf[:])
 

from contextlib import ExitStack

import concourse.mybir as mybir
from concourse.masks import make_identity

D, E, T, I, Q, G = 512, 512, 2048, 512, 256, 32
FLOPS = 2 * 2 * D * Q * I + 2 * I * E * Q

F32 = mybir.dt.float32
BF16 = mybir.dt.bfloat16
I32 = mybir.dt.int32
U32 = mybir.dt.uint32
U16 = mybir.dt.uint16
U8 = mybir.dt.uint8
FP8X4 = mybir.dt.float8_e4m3fn_x4
FP4X4 = mybir.dt.float4_e2m1fn_x4
ALU = mybir.AluOpType
ACT = mybir.ActivationFunctionType
AXIS = mybir.AxisListType

P = 128
PACK = 4
PAGE = I // G
ROW_TILES = Q // P


def tile_attend_ttpagegate_pl_kernel(tc, query, dquery, keys_words, keys_scales, th, steep, slot_factor, vals, offs, out_0, out_1, out_2):
    nc = tc.nc
    with ExitStack() as ctx:
        sb = ctx.enter_context(tc.tile_pool(name="sb", bufs=1))
        ps = ctx.enter_context(tc.psum_pool(name="ps", bufs=1))
        zp = ctx.enter_context(tc.tile_pool(name="zp", bufs=1))
        vp = ctx.enter_context(tc.tile_pool(name="vp", bufs=1))

        offsets = sb.tile([P, I // 16], U16, name="offsets")
        nc.sync.dma_start(offsets[:], offs)

        byte_pool = sb.tile([P, T], U8, name="byte_pool")
        nc.gpsimd.memset(byte_pool[:].bitcast(I32), 0)
        for quad in range(4):
            nc.sync.dma_start(byte_pool[:].bitcast(I32)[32 * quad : 32 * quad + 4, :], keys_scales[0].bitcast(I32)[4 * quad : 4 * quad + 4, :])
        key_pool = sb.tile([P, T], U16, name="key_pool")
        nc.sync.dma_start(key_pool[:].bitcast(I32), keys_words[0].bitcast(I32))

        row_numbers = sb.tile([P, P], F32, name="row_numbers")
        nc.vector.memset(row_numbers[:], 0.0)
        nc.sync.dma_start(row_numbers[0:2, :], th.rearrange("(k p) o -> k (p o)", p=P))
        nc.sync.dma_start(row_numbers[2:4, :], steep.rearrange("(k p) o -> k (p o)", p=P))

        raw = []
        for name, src in (("query", query), ("dquery", dquery)):
            t_raw = sb.tile([P, PACK, Q], F32, name=name + "_raw")
            nc.sync.dma_start(t_raw[:], src.rearrange("(p t) q -> p t q", t=PACK))
            raw.append(t_raw)

        os_sb = sb.tile([P, PACK], F32, name="os_sb")
        val_rows = vals.rearrange("(p t) c -> p t c", t=PACK)
        val_pool = [vp.tile([P, T], F32, name=f"val_pool{t}", offset=4 * T * t, align_bytes=64) for t in range(PACK)]
        halves = [slice(0, T // 2), slice(T // 2, T)]
        nc.sync.dma_start(val_pool[0][:, halves[0]], val_rows[:, 0, halves[0]])
        nc.sync.dma_start(val_pool[1][:], val_rows[:, 1, :])
        nc.sync.dma_start(val_pool[0][:, halves[1]], val_rows[:, 0, halves[1]])
        for t in range(2, PACK):
            nc.sync.dma_start(val_pool[t][:], val_rows[:, t, :])
        nc.sync.dma_start(os_sb[:], slot_factor.rearrange("o (p t) -> p (o t)", t=PACK))

        warm = sb.tile([P, 1], F32, name="warm")
        nc.gpsimd.memset(warm[:], 0.0)
        warmed = sb.tile([P, 1], F32, name="warmed")
        nc.scalar.activation(warmed[:], warm[:], ACT.Sigmoid)

        ident = sb.tile([P, P], F32, name="ident")
        make_identity(nc, ident[:])

        numbers = ps.tile([P, P], F32, name="numbers", tag="vbank0")
        nc.tensor.transpose(numbers[:], row_numbers[:], ident[:])
        slope = sb.tile([P, ROW_TILES], F32, name="slope")
        nslope = sb.tile([P, ROW_TILES], F32, name="nslope")
        th_sb = sb.tile([P, ROW_TILES], F32, name="th_sb")
        nc.scalar.activation(slope[:], numbers[:, 2:4], ACT.Copy, scale=1.0 / PAGE)
        nc.scalar.activation(nslope[:], numbers[:, 2:4], ACT.Copy, scale=-1.0 / PAGE)
        nc.scalar.activation(th_sb[:], numbers[:, 0:2], ACT.Copy, scale=float(PAGE))
        shift = sb.tile([P, ROW_TILES], F32, name="shift")
        nshift = sb.tile([P, ROW_TILES], F32, name="nshift")
        nc.vector.tensor_tensor(shift[:], slope[:], th_sb[:], ALU.mult)
        nc.vector.tensor_tensor(nshift[:], nslope[:], th_sb[:], ALU.mult)

        key_words = sb.tile([P, I], U16, name="key_words", align_bytes=64)
        key_bytes = sb.tile([P, I], U8, name="key_bytes", align_bytes=64)
        nc.vector.tensor_copy(key_bytes[:], byte_pool[:].indirect(offsets[:]))
        nc.vector.tensor_copy(key_words[:], key_pool[:].indirect(offsets[:]))

        score = [[None, None], [None, None]]
        for n in range(2):
            for k in range(ROW_TILES):
                grouped = sb.tile([P, P, PACK], BF16, name=f"q_grouped{n}{k}", align_bytes=64)
                dst = grouped[:].rearrange("p (c i) t -> p c t i", i=4)
                src = raw[n][:, :, k * P : (k + 1) * P].rearrange("p t (c i) -> p c t i", i=4)
                if (n, k) == (1, 1):
                    nc.vector.tensor_copy(dst, src)
                else:
                    nc.scalar.copy(dst, src)
                codes = sb.tile([P, P], U32, name=f"q_codes{n}{k}", align_bytes=64)
                scales = sb.tile([P, P], U8, name=f"q_scales{n}{k}", align_bytes=64)
                nc.vector.quantize_mx(out=codes[:].bitcast(FP8X4), scales=scales[:], in_=grouped[:].rearrange("p q t -> p (q t)"))
                bank = ps.tile([P, I], F32, name=f"score{n}{k}", tag=f"bank{n}{k}")
                nc.tensor.matmul_mx(out=bank[:], lhsT=codes[:].bitcast(FP8X4), lhsT_scale=scales[:],
                                    rhs=key_words[:].bitcast(FP4X4), rhs_scale=key_bytes[:], start=True, stop=True)
                score[n][k] = bank
        a, ta = score

        gate, shut = [], []
        page_sums = sb.tile([P, ROW_TILES, G], F32, name="page_sums", tag="sums_then_r")
        for k in range(ROW_TILES):
            s = page_sums[:, k, :]
            nc.vector.tensor_reduce(s, a[k][:].rearrange("q (g j) -> q g j", j=PAGE), AXIS.X, ALU.add)
            g4 = sb.tile([P, G, 4], F32, name=f"gate{k}")
            nc.scalar.activation(g4[:], s.rearrange("q (g o) -> q g o", o=1).to_broadcast([P, G, 4]), ACT.Sigmoid, bias=nshift[:, k : k + 1], scale=slope[:, k : k + 1])
            sh = sb.tile([P, G], F32, name=f"shut{k}")
            nc.scalar.activation(sh[:], s, ACT.Sigmoid, bias=shift[:, k : k + 1], scale=nslope[:, k : k + 1])
            gate.append(g4)
            shut.append(sh)

        r = []
        r_all = sb.tile([P, ROW_TILES, PACK, P], F32, name="r_all", tag="sums_then_r")
        for k in range(ROW_TILES):
            negmax = sb.tile([P, 1], F32, name=f"negmax{k}", tag="negmax0" if k == 0 else "then_picked0")
            nc.vector.tensor_reduce(negmax[:], a[k][:], AXIS.X, ALU.max, negate=True)
            rk = r_all[:, k, :, :]
            nc.scalar.activation(rk, a[k][:].rearrange("q (p t) -> q t p", t=PACK), ACT.Exp, bias=negmax[:])
            r.append(rk)

        def over_places(x):
            return x.rearrange("q g j -> q (g j)").rearrange("q (o p) -> q o p", o=1).to_broadcast([P, PACK, P])

        def after_gather(t, place, shape, dtype, name):
            return vp.tile(shape, dtype, name=name, offset=4 * T * t + 2048 * place, align_bytes=64)

        early_in = sb.tile([P, 4 * I], BF16, name="early_in", align_bytes=64)
        late_in = after_gather(3, 1, [P, 2 * I], BF16, "late_in")
        early_codes = after_gather(3, 0, [P, 4 * P], U32, "early_codes")
        late_codes = sb.tile([P, 2 * P], U32, name="late_codes", align_bytes=64)
        early_scales = sb.tile([P, 4 * P], U8, name="early_scales", align_bytes=64)
        late_scales = sb.tile([P, 2 * P], U8, name="late_scales", align_bytes=64)

        def operand(group, n):
            bf, codes, scales = group
            return bf[:, n * I : (n + 1) * I].rearrange("p (c t) -> p c t", t=PACK), codes[:, n * P : (n + 1) * P].bitcast(FP8X4), scales[:, n * P : (n + 1) * P]

        early, late = (early_in, early_codes, early_scales), (late_in, late_codes, late_scales)
        v_op = [operand(early, 0), operand(early, 1), operand(early, 2), operand(late, 0)]
        w_op = [operand(early, 3), operand(late, 1)]

        def values(t):
            if t in (1, 2):
                picked = zp.tile([P, I], BF16, name=f"picked{t}", offset=2048 + 1024 * (t - 1))
            else:
                picked = sb.tile([P, I], BF16, name=f"picked{t}", tag=f"then_picked{t}")
            if t == 0:
                rounded = sb.tile([P, T], BF16, name="rounded")
                for cols in halves:
                    nc.scalar.copy(rounded[:, cols], val_pool[t][:, cols])
                nc.scalar.activation(picked[:], rounded[:].indirect(offsets[:]), ACT.Copy)
            else:
                nc.vector.tensor_copy(picked[:], val_pool[t][:].indirect(offsets[:]))
            pairs = picked[:].bitcast(F32)
            turned = ps.tile([P, 2, P], F32, name=f"v_turned{t}", tag=f"vbank{t}")
            for u in range(2):
                nc.tensor.transpose(turned[:, u, :], pairs[:, u : I // 2 : 2], ident[:])
            nc.scalar.copy(v_op[t][0].bitcast(F32), turned[:].rearrange("p u e -> p e u"))

        def weights(k):
            ts = sb.tile([P, G], F32, name=f"ts{k}")
            nc.vector.tensor_reduce(ts[:], ta[k][:].rearrange("q (g j) -> q g j", j=PAGE), AXIS.X, ALU.add)
            h = sb.tile([P, G], F32, name=f"h{k}")
            nc.vector.scalar_tensor_tensor(h[:], ts[:], slope[:, k : k + 1], shut[k][:], ALU.mult, ALU.mult)
            zk = zp.tile([P, PACK, P], F32, name=f"z{k}", offset=2048 * k)
            nc.vector.tensor_tensor(zk[:].rearrange("q t (g j) -> q t g j", j=4), ta[k][:].rearrange("q (g j t) -> q t g j", t=PACK, j=4),
                                    h[:].rearrange("q (a g b) -> q a g b", a=1, b=1).to_broadcast([P, PACK, G, 4]), ALU.add)
            p = sb.tile([P, PACK, P], F32, name=f"p{k}")
            total = sb.tile([P, 1], F32, name=f"total{k}")
            nc.vector.scalar_tensor_tensor(p[:], r[k], 1.0, over_places(gate[k][:]), ALU.mult, ALU.mult, accum_out=total[:])
            inv = sb.tile([P, 1], F32, name=f"inv{k}", tag="inv0" if k == 0 else "then_picked3")
            nc.vector.reciprocal(inv[:], total[:])
            tp = sb.tile([P, PACK, P], F32, name=f"tp{k}")
            mean = sb.tile([P, 1], F32, name=f"mean{k}")
            nc.vector.scalar_tensor_tensor(tp[:], p[:], inv[:], zk[:], ALU.mult, ALU.mult, accum_out=mean[:])
            return p, inv, tp, mean

        def turn_weights(k, p, inv, tp, mean):
            ninv = sb.tile([P, 1], F32, name=f"ninv{k}")
            nc.scalar.activation(ninv[:], inv[:], ACT.Copy, scale=-1.0)
            back = sb.tile([P, 1], F32, name=f"back{k}")
            nc.scalar.activation(back[:], mean[:], ACT.Copy, scale=ninv[:])
            pk = sb.tile([P, PACK, P], F32, name=f"pk{k}")
            nc.scalar.activation(pk[:], p[:], ACT.Copy, scale=back[:])
            turned = ps.tile([P, PACK, P], F32, name=f"w_turned{k}", tag=f"bank0{k}")
            for t in range(PACK):
                nc.tensor.matmul(turned[:, t, :], tp[:, t, :], ident[:], start=True, stop=False, is_transpose=True)
                nc.tensor.matmul(turned[:, t, :], pk[:, t, :], ident[:], start=False, stop=True, is_transpose=True)
            return turned

        turned_w = [turn_weights(k, *weights(k)) for k in range(ROW_TILES)]
        for t in range(PACK):
            values(t)
        for k in range(ROW_TILES):
            nc.vector.tensor_tensor(w_op[k][0], turned_w[k][:].rearrange("p t q -> p q t"),
                                    os_sb[:].rearrange("p (o t) -> p o t", o=1).to_broadcast([P, P, PACK]), ALU.mult)
        for bf, codes, scales in (early, late):
            nc.vector.quantize_mx(out=codes[:].bitcast(FP8X4), scales=scales[:], in_=bf[:])

        o_codes = sb.tile([P, Q], U32, name="o_codes", align_bytes=64)
        o_scales = sb.tile([P, Q], U8, name="o_scales", align_bytes=64)
        for k in range(ROW_TILES):
            rows = slice(k * P, (k + 1) * P)
            o = sb.tile([P, PACK, P], F32, name=f"o{k}")
            cut = 3 if k == 0 else 2
            for first, last, tag in ((0, cut, f"bank1{k}"), (cut, PACK, f"vbank{k}")):
                acc = ps.tile([P, last - first, P], F32, name=f"acc{k}{first}", tag=tag)
                for t in range(first, last):
                    nc.tensor.matmul_mx(out=acc[:, t - first, :], lhsT=v_op[t][1], lhsT_scale=v_op[t][2],
                                        rhs=w_op[k][1], rhs_scale=w_op[k][2], start=True, stop=True)
                if (k, first) == (1, 0):
                    nc.vector.tensor_copy(o[:, first:last, :], acc[:])
                else:
                    nc.scalar.copy(o[:, first:last, :], acc[:])
            nc.sync.dma_start(out_0.rearrange("(p t) q -> p t q", t=PACK)[:, :, rows], o[:])
            grouped = sb.tile([P, P, PACK], BF16, name=f"o_grouped{k}", align_bytes=64)
            nc.vector.tensor_copy(grouped[:].rearrange("p (c i) t -> p c t i", i=4), o[:].rearrange("p t (c i) -> p c t i", i=4))
            nc.vector.quantize_mx(out=o_codes[:, rows].bitcast(FP8X4), scales=o_scales[:, rows], in_=grouped[:].rearrange("p q t -> p (q t)"))
        nc.sync.dma_start(out_1[0].rearrange("p q t -> p (q t)").bitcast(I32), o_codes[:].bitcast(I32))
        for quad in range(4):
            eng = nc.sync if quad % 2 == 0 else nc.scalar
            eng.dma_start(out_2[0].bitcast(I32)[4 * quad : 4 * quad + 4, :], o_scales[:].bitcast(I32)[32 * quad : 32 * quad + 4, :])
